import numpy as np
import ml_dtypes


def mxq(x, axis, fmt="e4m3"):
    dtype, down = {"e4m3": (ml_dtypes.float8_e4m3fn, 7), "e5m2": (ml_dtypes.float8_e5m2, 14)}[fmt]
    v = np.moveaxis(np.asarray(x, np.float32).astype(ml_dtypes.bfloat16).astype(np.float64), axis, -1)
    blocks = v.reshape(v.shape[:-1] + (-1, 32))
    amax = np.abs(blocks).max(-1, keepdims=True)
    byte = np.maximum(np.where(amax > 0, np.frexp(amax)[1] - 1 + 127, 0) - down, 1)
    scale = np.exp2(byte - 127.0)
    codes = (blocks / scale).astype(np.float32).astype(dtype).astype(np.float64)
    return np.moveaxis((codes * scale).reshape(v.shape), -1, axis)


WIDE = False


def mx_kscale(k):
    if not WIDE:
        return np.ones(k)
    levels = np.array([10, -10, 5, -5, 0])
    if k % 512:
        return np.exp2(np.random.permutation(np.resize(levels, k // 32))).repeat(32)
    a = np.empty((k // 512, 16))
    for p in range(k // 512):
        a[p, :8] = np.random.permutation(np.resize(levels, 8))
        for g in range(8):
            far = levels[np.abs(levels - a[p, g]) >= 10]
            a[p, g + 8] = far[np.random.randint(len(far))]
    return np.exp2(a.ravel()).repeat(32)


BF16 = ml_dtypes.bfloat16


def bf(x):
    return np.asarray(x, np.float32).astype(BF16)


def f64(x):
    return np.asarray(x).astype(np.float64)


B, H, T, S, E = 4, 4, 512, 512, 128


def draw0():
    t = mx_kscale(S)
    return {"q": bf(np.random.standard_normal((B, H, T, E))),
            "k": bf(np.random.standard_normal((B, H, S, E))),
            "v": bf(np.random.standard_normal((B, H, S, E)) / t[:, None]),
            "mixl": bf(np.random.standard_normal((H, H)) / np.sqrt(H)),
            "mixw": bf(np.random.standard_normal((H, H)) / np.sqrt(H)),
            "gs": bf((1.0 + 0.1 * np.random.standard_normal(S)) * t)}


def mix_heads(x, w):
    return np.sum(w[None, :, :, None, None] * x[:, :, None, :, :], axis=1)


def core(q, k, v, mixl, mixw, gs):
    l = f64(q) @ f64(k).transpose(0, 1, 3, 2) / np.sqrt(E)
    m = mix_heads(l, f64(mixl))
    e = np.exp(m - m.max(-1, keepdims=True))
    p = e / e.sum(-1, keepdims=True)
    c = mix_heads(p, f64(mixw))
    u = np.sqrt(S) * c * f64(gs)[None, None, None, :]
    return mxq(u, 3, "e4m3") @ mxq(f64(v), 2, "e4m3")


def e4m3fn_bytes(y):
    return np.clip(np.asarray(y, np.float64), -448.0, 448.0).astype(np.float32).astype(ml_dtypes.float8_e4m3fn).view(np.uint8)


def e4m3fn_values(b):
    return np.asarray(b, np.uint8).view(ml_dtypes.float8_e4m3fn).astype(np.float64)


def setup_inputs():
    d = draw0()
    x0 = np.asarray(d['v']).astype(np.float64)
    s = (np.max(np.abs(x0), axis=(0, 1, 3), keepdims=True) / 448.0).astype(np.float32)
    out = {}
    for k, v in d.items():
        if k == 'v':
            out['v_bytes'] = e4m3fn_bytes(x0 / s.astype(np.float64))
            out['v_scale'] = s
        else:
            out[k] = v
    return out


def reference(q, k, v_bytes, v_scale, mixl, mixw, gs):
    return core(q, k, e4m3fn_values(v_bytes) * v_scale.astype(np.float64), mixl, mixw, gs)

@@ -1,0 +1,359 @@
+from contextlib import ExitStack
+
+import concourse.mybir as mybir
+from concourse.masks import make_identity
+
+B, H, T, S, E = 4, 4, 512, 512, 128
+P = 128
+SLOTS = 4
+
+F32 = mybir.dt.float32
+BF16 = mybir.dt.bfloat16
+U32 = mybir.dt.uint32
+U8 = mybir.dt.uint8
+FP8 = mybir.dt.float8_e4m3fn
+FP8X4 = mybir.dt.float8_e4m3fn_x4
+ACT = mybir.ActivationFunctionType
+ALU = mybir.AluOpType
+AX = mybir.AxisListType
+
+FLOPS = 2 * 2 * B * H * T * S * E
+
+STEPS = B * SLOTS
+SCALAR_HEADS = (3,)
+V_AT, V_EVERY = 11, 5
+BUFS = {"lt": 4, "m": 2, "u": 2}
+TURN_TAG, O_TAG = "lt", "lt"
+
+ORDER = (
+    ("mx_product", 14),
+    ("store", 15),
+    ("logits", 0),
+    ("row_max", 4),
+    ("quantise", 11),
+    ("gain", 10),
+    ("scale_first", 0),
+    ("add_second", 0),
+    ("transpose_qk", -20),
+    ("mixed_logits", 3),
+    ("mixed_weights", 9),
+    ("exponentials", 4),
+    ("weighted", 8),
+    ("weights", 4),
+)
+
+
+def tile_caittalkingheadsattention_kernel(tc, q, k, v_bytes, v_scale, mixl, mixw, gs, out):
+    nc = tc.nc
+    with ExitStack() as ctx:
+        const = ctx.enter_context(tc.tile_pool(name="const", bufs=1))
+        load = ctx.enter_context(tc.tile_pool(name="load", bufs=2))
+        work = ctx.enter_context(tc.tile_pool(name="work", bufs=2))
+        psum = ctx.enter_context(tc.psum_pool(name="psum", bufs=2))
+        ctx.enter_context(tc.manual_schedule())
+
+        raw = {}
+
+        def load_qk(b):
+            for h in range(H):
+                for name, src in (("k", k), ("q", q)):
+                    t = load.tile([P, SLOTS, E], BF16, name="raw_" + name + str(h), tag="raw_" + name + str(h), bufs=2)
+                    nc.sync.dma_start(out=t[:], in_=src[b, h].rearrange("(p r) e -> p r e", r=SLOTS))
+                    raw[name, b, h] = t
+
+        load_qk(0)
+        wl_bf = const.tile([P, H * H], BF16, name="wl_bf")
+        nc.sync.dma_start(out=wl_bf[:], in_=mixl.rearrange("h j -> (h j)").partition_broadcast(P))
+        wm_bf = const.tile([P, H * H], BF16, name="wm_bf")
+        nc.sync.dma_start(out=wm_bf[:], in_=mixw.rearrange("h j -> (h j)").partition_broadcast(P))
+        gs_bf = const.tile([P, SLOTS], BF16, name="gs_bf")
+        nc.sync.dma_start(out=gs_bf[:], in_=gs.rearrange("(p r) -> p r", r=SLOTS))
+        vs = const.tile([P, SLOTS], F32, name="vs")
+        nc.sync.dma_start(out=vs[:], in_=v_scale[0, 0].rearrange("(p r) c -> p (r c)", r=SLOTS))
+        v8 = []
+        for b in range(B):
+            t = const.tile([P, SLOTS, H, E], U8, name="v8_" + str(b))
+            for r in range(SLOTS):
+                nc.sync.dma_start(out=t[:, r], in_=v_bytes[b].rearrange("h (p r) e -> p r h e", r=SLOTS)[:, r])
+            v8.append(t)
+
+        load_qk(1)
+
+        ident = const.tile([P, P], F32, name="ident")
+        make_identity(nc, ident[:])
+        ident_bf = const.tile([P, P], BF16, name="ident_bf")
+        nc.vector.tensor_copy(out=ident_bf[:], in_=ident[:])
+        wl = const.tile([P, H * H], F32, name="wl")
+        nc.vector.tensor_scalar(out=wl[:], in0=wl_bf[:], scalar1=1.0 / E**0.5, scalar2=None, op0=ALU.mult)
+        wm = const.tile([P, H, H], F32, name="wm")
+        nc.vector.tensor_copy(out=wm[:].rearrange("p h j -> p (h j)"), in_=wm_bf[:])
+        gain = const.tile([P, SLOTS], F32, name="gain")
+        nc.vector.tensor_scalar(out=gain[:], in0=gs_bf[:], scalar1=S**0.5, scalar2=None, op0=ALU.mult)
+        gains = const.tile([P, P, SLOTS], F32, name="gains")
+        nc.vector.tensor_copy(out=gains[:], in_=gain[:].unsqueeze(1).to_broadcast([P, P, SLOTS]))
+
+        v_wide = {}
+        v_grouped = {}
+        v_codes = {}
+        v_scales = {}
+
+        def widen_v(b):
+            t = work.tile([P, SLOTS, H * E], BF16, name="v_wide", tag="v_wide", bufs=2)
+            for r in range(SLOTS):
+                nc.vector.tensor_scalar(
+                    out=t[:, r],
+                    in0=v8[b][:, r].rearrange("p h e -> p (h e)").bitcast(FP8),
+                    scalar1=vs[:, r : r + 1],
+                    scalar2=None,
+                    op0=ALU.mult,
+                )
+            v_wide[b] = t
+
+        def group_v(b):
+            t = work.tile([P, H * E, SLOTS], BF16, name="v_grouped", tag="v_grouped", bufs=2, align_bytes=64)
+            nc.gpsimd.tensor_scalar(
+                out=t[:],
+                in0=v_wide[b][:].rearrange("p r n -> p n r"),
+                scalar1=1.0,
+                scalar2=0.0,
+                op0=ALU.mult,
+                op1=ALU.add,
+            )
+            v_grouped[b] = t
+
+        def quantise_v(b):
+            codes = const.tile([P, H * E], U32, name="v_codes" + str(b), align_bytes=64)
+            scales = const.tile([P, H * E], U8, name="v_scales" + str(b), align_bytes=64)
+            nc.vector.quantize_mx(
+                out=codes[:].bitcast(FP8X4), scales=scales[:], in_=v_grouped[b][:].rearrange("p n r -> p (n r)")
+            )
+            v_codes[b] = codes
+            v_scales[b] = scales
+
+        turned = {}
+        lt = {}
+        half = {}
+        mixed = {}
+        nmax = {}
+        expo = {}
+        rowsum = {}
+        wts = {}
+        prod = {}
+        upsum = {}
+        ub = {}
+        uq = {}
+        res = {}
+
+        def turn(b, h, name, engine):
+            bank = psum.tile([P, SLOTS, P], BF16, name="turn_bank", tag=TURN_TAG, bufs=BUFS[TURN_TAG])
+            for r in range(SLOTS):
+                nc.tensor.transpose(bank[:, r], raw[name, b, h][:, r], ident_bf[:])
+            t = load.tile([P, SLOTS, P], BF16, name="turned_" + name + str(h), tag="turned_" + name + str(h), bufs=2)
+            if engine == "v":
+                nc.vector.tensor_copy(out=t[:], in_=bank[:])
+            else:
+                nc.scalar.copy(out=t[:], in_=bank[:])
+            turned[name, b, h] = t
+
+        def transpose_qk(s, r):
+            n = (s % SLOTS) * 4 + r
+            b = s // SLOTS
+            if b == 0:
+                return
+            if n % 2 == 1:
+                turn(b, n // 4, "k" if n % 4 == 1 else "q", "s")
+            if n == 15 and b + 1 < B:
+                load_qk(b + 1)
+
+        def logits(s, r):
+            if r % 2:
+                return
+            b, i = s // SLOTS, s % SLOTS
+            for h in (r, r + 1):
+                bank = psum.tile([P, SLOTS, P], F32, name="lt", tag="lt", bufs=BUFS["lt"])
+                for x in range(SLOTS):
+                    nc.tensor.matmul(
+                        out=bank[:, x],
+                        lhsT=turned["k", b, h][:, x],
+                        rhs=turned["q", b, h][:, i],
+                        start=True,
+                        stop=True,
+                    )
+                lt[s, h] = bank
+
+        def scale_first(s, r):
+            h = r // 2 * 2
+            for j in (r % 2 * 2, r % 2 * 2 + 1):
+                t = work.tile([P, SLOTS * P], F32, name="half", tag="half" + str(h) + str(j), bufs=2)
+                nc.scalar.activation(
+                    out=t[:],
+                    in_=lt[s, h][:].rearrange("p r t -> p (r t)"),
+                    func=ACT.Copy,
+                    scale=wl[:, H * h + j : H * h + j + 1],
+                )
+                half[s, h, j] = t
+
+        def add_second(s, r):
+            h = r // 2 * 2
+            for j in (r % 2 * 2, r % 2 * 2 + 1):
+                t = half[s, h, j]
+                nc.vector.scalar_tensor_tensor(
+                    out=t[:],
+                    in0=lt[s, h + 1][:].rearrange("p r t -> p (r t)"),
+                    scalar=wl[:, H * (h + 1) + j : H * (h + 1) + j + 1],
+                    in1=t[:],
+                    op0=ALU.mult,
+                    op1=ALU.add,
+                )
+
+        def mixed_logits(s, j):
+            bank = psum.tile([P, SLOTS, P], F32, name="m_bank", tag="m", bufs=BUFS["m"])
+            for x in range(SLOTS):
+                for h in (0, 2):
+                    nc.tensor.matmul(
+                        out=bank[:, x],
+                        lhsT=half[s, h, j][:, x * P : (x + 1) * P],
+                        rhs=ident[:],
+                        start=(h == 0),
+                        stop=(h == 2),
+                        is_transpose=True,
+                    )
+            mixed[s, j] = bank
+
+        def row_max(s, j):
+            if j == 0:
+                nmax[s] = work.tile([P, H], F32, name="nmax", tag="nmax", bufs=3)
+            nc.vector.tensor_reduce(
+                out=nmax[s][:, j : j + 1],
+                in_=mixed[s, j][:].rearrange("p r t -> p (r t)"),
+                axis=AX.X,
+                op=ALU.max,
+                negate=True,
+            )
+
+        def exponentials(s, j):
+            if j == 0:
+                rowsum[s] = work.tile([P, H], F32, name="rowsum", tag="rowsum", bufs=3)
+            t = work.tile([P, SLOTS * P], F32, name="expo", tag="expo" + str(j), bufs=2)
+            nc.scalar.activation(
+                out=t[:],
+                in_=mixed[s, j][:].rearrange("p r t -> p (r t)"),
+                func=ACT.Exp,
+                bias=nmax[s][:, j : j + 1],
+                accum_out=rowsum[s][:, j : j + 1],
+            )
+            expo[s, j] = t
+
+        def weights(s, r):
+            if r < 3:
+                return
+            inv = work.tile([P, H], F32, name="inv", tag="inv", bufs=2)
+            nc.vector.reciprocal(out=inv[:], in_=rowsum[s][:])
+            w = work.tile([P, H, H], F32, name="w", tag="w", bufs=2)
+            nc.vector.tensor_tensor(
+                out=w[:], in0=wm[:], in1=inv[:].unsqueeze(2).to_broadcast([P, H, H]), op=ALU.mult
+            )
+            wts[s] = w
+
+        def weighted(s, j):
+            for h in range(H):
+                t = work.tile([P, SLOTS * P], F32, name="prod", tag="prod" + str(h), bufs=6)
+                col = wts[s][:, h, j : j + 1]
+                if h in SCALAR_HEADS:
+                    nc.scalar.activation(out=t[:], in_=expo[s, h][:], func=ACT.Copy, scale=col)
+                else:
+                    nc.gpsimd.tensor_scalar(
+                        out=t[:], in0=expo[s, h][:], scalar1=col, scalar2=0.0, op0=ALU.mult, op1=ALU.add
+                    )
+                prod[s, h, j] = t
+
+        def mixed_weights(s, j):
+            bank = psum.tile([P, SLOTS, P], F32, name="u_bank", tag="u", bufs=BUFS["u"])
+            for x in range(SLOTS):
+                for h in range(H):
+                    nc.tensor.matmul(
+                        out=bank[:, x],
+                        lhsT=prod[s, h, j][:, x * P : (x + 1) * P],
+                        rhs=ident[:],
+                        start=(h == 0),
+                        stop=(h == H - 1),
+                        is_transpose=True,
+                    )
+            upsum[s, j] = bank
+
+        def gain_stage(s, j):
+            if j == 0:
+                ub[s] = work.tile([P, H, P, SLOTS], BF16, name="ub", tag="ub", bufs=2, align_bytes=64)
+            nc.vector.tensor_tensor(
+                out=ub[s][:, j],
+                in0=upsum[s, j][:].rearrange("p r t -> p t r"),
+                in1=gains[:],
+                op=ALU.mult,
+            )
+
+        def quantise(s, r):
+            if r < 3:
+                return
+            codes = work.tile([P, H * P], U32, name="u_codes", tag="u_codes", bufs=2, align_bytes=64)
+            scales = work.tile([P, H * P], U8, name="u_scales", tag="u_scales", bufs=2, align_bytes=64)
+            nc.vector.quantize_mx(
+                out=codes[:].bitcast(FP8X4), scales=scales[:], in_=ub[s][:].rearrange("p h t r -> p (h t r)")
+            )
+            uq[s] = (codes, scales)
+
+        def mx_product(s, r):
+            if r < 3:
+                return
+            b = s // SLOTS
+            codes, scales = uq[s]
+            bank = psum.tile([P, H, E], F32, name="o_bank", tag=O_TAG, bufs=BUFS[O_TAG])
+            for j in range(H):
+                nc.tensor.matmul_mx(
+                    out=bank[:, j],
+                    lhsT=codes[:, j * P : (j + 1) * P].bitcast(FP8X4),
+                    lhsT_scale=scales[:, j * P : (j + 1) * P],
+                    rhs=v_codes[b][:, j * E : (j + 1) * E].bitcast(FP8X4),
+                    rhs_scale=v_scales[b][:, j * E : (j + 1) * E],
+                    start=True,
+                    stop=True,
+                )
+            res[s] = bank
+
+        def store(s, r):
+            if r < 3:
+                return
+            b, i = s // SLOTS, s % SLOTS
+            t = work.tile([P, H, E], F32, name="o_tile", tag="o_tile", bufs=3)
+            nc.scalar.copy(out=t[:], in_=res[s][:])
+            nc.sync.dma_start(out=out[b].rearrange("j (p i) e -> p i j e", i=SLOTS)[:, i], in_=t[:])
+
+        for h in range(H):
+            turn(0, h, "k", "v")
+            turn(0, h, "q", "s")
+
+        stages = {
+            "transpose_qk": transpose_qk,
+            "logits": logits,
+            "mx_product": mx_product,
+            "mixed_logits": mixed_logits,
+            "mixed_weights": mixed_weights,
+            "scale_first": scale_first,
+            "exponentials": exponentials,
+            "weighted": weighted,
+            "store": store,
+            "gain": gain_stage,
+            "row_max": row_max,
+            "add_second": add_second,
+            "weights": weights,
+            "quantise": quantise,
+        }
+        first = min(offset for name, offset in ORDER)
+        last = max(offset for name, offset in ORDER)
+        for g in range(first, 4 * STEPS + last):
+            for stage, offset in ((widen_v, V_AT), (group_v, V_AT + 1), (quantise_v, V_AT + 3)):
+                if (g - offset) % V_EVERY == 0 and 0 <= (g - offset) // V_EVERY < B:
+                    stage((g - offset) // V_EVERY)
+            for name, offset in ORDER:
+                n = g - offset
+                if 0 <= n < 4 * STEPS:
+                    stages[name](n // 4, n % 4)

@@ -20,26 +20,33 @@ AX = mybir.AxisListType
 FLOPS = 2 * 2 * B * H * T * S * E
 
 STEPS = B * SLOTS
-SCALAR_HEADS = (3,)
-V_AT, V_EVERY = 11, 5
+SPLIT = ("svvs", "svvs", "svvs", "svvv")
+SPLIT_END = ("svvs", "svvs", "svvs", "svvv")
+N_END = 1
+
+
+def who_scales(s, h, j):
+    return (SPLIT_END if s >= STEPS - N_END else SPLIT)[j][h]
+
+V_AT, V_EVERY = 1, 2
 BUFS = {"lt": 4, "m": 2, "u": 2}
 TURN_TAG, O_TAG = "lt", "lt"
 
 ORDER = (
-    ("mx_product", 14),
-    ("store", 15),
-    ("logits", 0),
     ("row_max", 4),
-    ("quantise", 11),
     ("gain", 10),
+    ("transpose_qk", -13),
+    ("logits", 0),
+    ("store", 15),
     ("scale_first", 0),
     ("add_second", 0),
-    ("transpose_qk", -20),
+    ("weighted", 8),
+    ("mx_product", 14),
+    ("quantise", 10),
+    ("exponentials", 4),
+    ("weights", 4),
     ("mixed_logits", 3),
     ("mixed_weights", 9),
-    ("exponentials", 4),
-    ("weighted", 8),
-    ("weights", 4),
 )
 
 
@@ -158,10 +165,9 @@ def tile_caittalkingheadsattention_kernel(tc, q, k, v_bytes, v_scale, mixl, mixw
         def transpose_qk(s, r):
             n = (s % SLOTS) * 4 + r
             b = s // SLOTS
-            if b == 0:
+            if b == 0 or n < 8:
                 return
-            if n % 2 == 1:
-                turn(b, n // 4, "k" if n % 4 == 1 else "q", "s")
+            turn(b, (n - 8) // 2, "k" if n % 2 == 0 else "q", "s")
             if n == 15 and b + 1 < B:
                 load_qk(b + 1)
 
@@ -259,8 +265,13 @@ def tile_caittalkingheadsattention_kernel(tc, q, k, v_bytes, v_scale, mixl, mixw
             for h in range(H):
                 t = work.tile([P, SLOTS * P], F32, name="prod", tag="prod" + str(h), bufs=6)
                 col = wts[s][:, h, j : j + 1]
-                if h in SCALAR_HEADS:
+                who = who_scales(s, h, j)
+                if who == "s":
                     nc.scalar.activation(out=t[:], in_=expo[s, h][:], func=ACT.Copy, scale=col)
+                elif who == "v":
+                    nc.vector.tensor_scalar(
+                        out=t[:], in0=expo[s, h][:], scalar1=col, scalar2=None, op0=ALU.mult
+                    )
                 else:
                     nc.gpsimd.tensor_scalar(
                         out=t[:], in0=expo[s, h][:], scalar1=col, scalar2=0.0, op0=ALU.mult, op1=ALU.add

@@ -20,33 +20,36 @@ AX = mybir.AxisListType
 FLOPS = 2 * 2 * B * H * T * S * E
 
 STEPS = B * SLOTS
-SPLIT = ("svvs", "svvs", "svvs", "svvv")
-SPLIT_END = ("svvs", "svvs", "svvs", "svvv")
-N_END = 1
+SPLIT = ("gggs", "ggsg", "gggg", "sggs")
+SPLIT_END = ("ggvs", "ssvs", "svvs", "svvg")
+N_END = 2
+WARM = 96
 
 
 def who_scales(s, h, j):
     return (SPLIT_END if s >= STEPS - N_END else SPLIT)[j][h]
 
-V_AT, V_EVERY = 1, 2
-BUFS = {"lt": 4, "m": 2, "u": 2}
-TURN_TAG, O_TAG = "lt", "lt"
+V_AT, V_EVERY = 2, 5
+BUFS = {"lt": 3, "m": 2, "u": 3}
+TURN_TAG, O_TAG = "u", "m"
 
 ORDER = (
+    ("mx_product", 15),
+    ("store", 16),
+    ("mix_weights_a", 10),
+    ("weights", 5),
+    ("gain", 11),
     ("row_max", 4),
-    ("gain", 10),
-    ("transpose_qk", -13),
-    ("logits", 0),
-    ("store", 15),
-    ("scale_first", 0),
-    ("add_second", 0),
-    ("weighted", 8),
-    ("mx_product", 14),
-    ("quantise", 10),
+    ("mix_weights_b", 10),
+    ("scale_first", -1),
+    ("logits_a", -2),
     ("exponentials", 4),
-    ("weights", 4),
+    ("weighted", 8),
+    ("logits_b", -2),
+    ("transpose_qk", -15),
     ("mixed_logits", 3),
-    ("mixed_weights", 9),
+    ("add_second", 0),
+    ("quantise", 11),
 )
 
 
@@ -171,21 +174,24 @@ def tile_caittalkingheadsattention_kernel(tc, q, k, v_bytes, v_scale, mixl, mixw
             if n == 15 and b + 1 < B:
                 load_qk(b + 1)
 
-        def logits(s, r):
-            if r % 2:
-                return
+        def logits(s, h, slots):
             b, i = s // SLOTS, s % SLOTS
-            for h in (r, r + 1):
-                bank = psum.tile([P, SLOTS, P], F32, name="lt", tag="lt", bufs=BUFS["lt"])
-                for x in range(SLOTS):
-                    nc.tensor.matmul(
-                        out=bank[:, x],
-                        lhsT=turned["k", b, h][:, x],
-                        rhs=turned["q", b, h][:, i],
-                        start=True,
-                        stop=True,
-                    )
-                lt[s, h] = bank
+            if slots[0] == 0:
+                lt[s, h] = psum.tile([P, SLOTS, P], F32, name="lt", tag="lt", bufs=BUFS["lt"])
+            for x in slots:
+                nc.tensor.matmul(
+                    out=lt[s, h][:, x],
+                    lhsT=turned["k", b, h][:, x],
+                    rhs=turned["q", b, h][:, i],
+                    start=True,
+                    stop=True,
+                )
+
+        def logits_a(s, h):
+            logits(s, h, (0, 1))
+
+        def logits_b(s, h):
+            logits(s, h, (2, 3))
 
         def scale_first(s, r):
             h = r // 2 * 2
@@ -278,19 +284,33 @@ def tile_caittalkingheadsattention_kernel(tc, q, k, v_bytes, v_scale, mixl, mixw
                     )
                 prod[s, h, j] = t
 
-        def mixed_weights(s, j):
-            bank = psum.tile([P, SLOTS, P], F32, name="u_bank", tag="u", bufs=BUFS["u"])
-            for x in range(SLOTS):
+        def mix_weights(s, j, slots):
+            if slots[0] == 0:
+                upsum[s, j] = psum.tile([P, SLOTS, P], F32, name="u_bank", tag="u", bufs=BUFS["u"])
+            for x in slots:
                 for h in range(H):
                     nc.tensor.matmul(
-                        out=bank[:, x],
+                        out=upsum[s, j][:, x],
                         lhsT=prod[s, h, j][:, x * P : (x + 1) * P],
                         rhs=ident[:],
                         start=(h == 0),
                         stop=(h == H - 1),
                         is_transpose=True,
                     )
-            upsum[s, j] = bank
+                if x == 1:
+                    nc.tensor.matmul(
+                        out=upsum[s, j][:, 3, :WARM],
+                        lhsT=ident[:],
+                        rhs=ident[:, :WARM],
+                        start=True,
+                        stop=True,
+                    )
+
+        def mix_weights_a(s, j):
+            mix_weights(s, j, (0, 1))
+
+        def mix_weights_b(s, j):
+            mix_weights(s, j, (2, 3))
 
         def gain_stage(s, j):
             if j == 0:
@@ -344,10 +364,12 @@ def tile_caittalkingheadsattention_kernel(tc, q, k, v_bytes, v_scale, mixl, mixw
 
         stages = {
             "transpose_qk": transpose_qk,
-            "logits": logits,
+            "logits_a": logits_a,
+            "logits_b": logits_b,
             "mx_product": mx_product,
             "mixed_logits": mixed_logits,
-            "mixed_weights": mixed_weights,
+            "mix_weights_a": mix_weights_a,
+            "mix_weights_b": mix_weights_b,
             "scale_first": scale_first,
             "exponentials": exponentials,
             "weighted": weighted,

from contextlib import ExitStack

import concourse.mybir as mybir
from concourse.masks import make_identity

B, H, T, S, E = 4, 4, 512, 512, 128
P = 128
SLOTS = 4

F32 = mybir.dt.float32
BF16 = mybir.dt.bfloat16
U32 = mybir.dt.uint32
U8 = mybir.dt.uint8
FP8 = mybir.dt.float8_e4m3fn
FP8X4 = mybir.dt.float8_e4m3fn_x4
ACT = mybir.ActivationFunctionType
ALU = mybir.AluOpType
AX = mybir.AxisListType

FLOPS = 2 * 2 * B * H * T * S * E

STEPS = B * SLOTS
SPLIT = ("gggs", "ggsg", "gggg", "sggs")
SPLIT_END = ("ggvs", "ssvs", "svvs", "svvg")
N_END = 2
WARM = 96


def who_scales(s, h, j):
    return (SPLIT_END if s >= STEPS - N_END else SPLIT)[j][h]

V_AT, V_EVERY = 2, 5
BUFS = {"lt": 3, "m": 2, "u": 3}
TURN_TAG, O_TAG = "u", "m"

ORDER = (
    ("mx_product", 15),
    ("store", 16),
    ("mix_weights_a", 10),
    ("weights", 5),
    ("gain", 11),
    ("row_max", 4),
    ("mix_weights_b", 10),
    ("scale_first", -1),
    ("logits_a", -2),
    ("exponentials", 4),
    ("weighted", 8),
    ("logits_b", -2),
    ("transpose_qk", -15),
    ("mixed_logits", 3),
    ("add_second", 0),
    ("quantise", 11),
)


def tile_caittalkingheadsattention_kernel(tc, q, k, v_bytes, v_scale, mixl, mixw, gs, out):
    nc = tc.nc
    with ExitStack() as ctx:
        const = ctx.enter_context(tc.tile_pool(name="const", bufs=1))
        load = ctx.enter_context(tc.tile_pool(name="load", bufs=2))
        work = ctx.enter_context(tc.tile_pool(name="work", bufs=2))
        psum = ctx.enter_context(tc.psum_pool(name="psum", bufs=2))
        ctx.enter_context(tc.manual_schedule())

        raw = {}

        def load_qk(b):
            for h in range(H):
                for name, src in (("k", k), ("q", q)):
                    t = load.tile([P, SLOTS, E], BF16, name="raw_" + name + str(h), tag="raw_" + name + str(h), bufs=2)
                    nc.sync.dma_start(out=t[:], in_=src[b, h].rearrange("(p r) e -> p r e", r=SLOTS))
                    raw[name, b, h] = t

        load_qk(0)
        wl_bf = const.tile([P, H * H], BF16, name="wl_bf")
        nc.sync.dma_start(out=wl_bf[:], in_=mixl.rearrange("h j -> (h j)").partition_broadcast(P))
        wm_bf = const.tile([P, H * H], BF16, name="wm_bf")
        nc.sync.dma_start(out=wm_bf[:], in_=mixw.rearrange("h j -> (h j)").partition_broadcast(P))
        gs_bf = const.tile([P, SLOTS], BF16, name="gs_bf")
        nc.sync.dma_start(out=gs_bf[:], in_=gs.rearrange("(p r) -> p r", r=SLOTS))
        vs = const.tile([P, SLOTS], F32, name="vs")
        nc.sync.dma_start(out=vs[:], in_=v_scale[0, 0].rearrange("(p r) c -> p (r c)", r=SLOTS))
        v8 = []
        for b in range(B):
            t = const.tile([P, SLOTS, H, E], U8, name="v8_" + str(b))
            for r in range(SLOTS):
                nc.sync.dma_start(out=t[:, r], in_=v_bytes[b].rearrange("h (p r) e -> p r h e", r=SLOTS)[:, r])
            v8.append(t)

        load_qk(1)

        ident = const.tile([P, P], F32, name="ident")
        make_identity(nc, ident[:])
        ident_bf = const.tile([P, P], BF16, name="ident_bf")
        nc.vector.tensor_copy(out=ident_bf[:], in_=ident[:])
        wl = const.tile([P, H * H], F32, name="wl")
        nc.vector.tensor_scalar(out=wl[:], in0=wl_bf[:], scalar1=1.0 / E**0.5, scalar2=None, op0=ALU.mult)
        wm = const.tile([P, H, H], F32, name="wm")
        nc.vector.tensor_copy(out=wm[:].rearrange("p h j -> p (h j)"), in_=wm_bf[:])
        gain = const.tile([P, SLOTS], F32, name="gain")
        nc.vector.tensor_scalar(out=gain[:], in0=gs_bf[:], scalar1=S**0.5, scalar2=None, op0=ALU.mult)
        gains = const.tile([P, P, SLOTS], F32, name="gains")
        nc.vector.tensor_copy(out=gains[:], in_=gain[:].unsqueeze(1).to_broadcast([P, P, SLOTS]))

        v_wide = {}
        v_grouped = {}
        v_codes = {}
        v_scales = {}

        def widen_v(b):
            t = work.tile([P, SLOTS, H * E], BF16, name="v_wide", tag="v_wide", bufs=2)
            for r in range(SLOTS):
                nc.vector.tensor_scalar(
                    out=t[:, r],
                    in0=v8[b][:, r].rearrange("p h e -> p (h e)").bitcast(FP8),
                    scalar1=vs[:, r : r + 1],
                    scalar2=None,
                    op0=ALU.mult,
                )
            v_wide[b] = t

        def group_v(b):
            t = work.tile([P, H * E, SLOTS], BF16, name="v_grouped", tag="v_grouped", bufs=2, align_bytes=64)
            nc.gpsimd.tensor_scalar(
                out=t[:],
                in0=v_wide[b][:].rearrange("p r n -> p n r"),
                scalar1=1.0,
                scalar2=0.0,
                op0=ALU.mult,
                op1=ALU.add,
            )
            v_grouped[b] = t

        def quantise_v(b):
            codes = const.tile([P, H * E], U32, name="v_codes" + str(b), align_bytes=64)
            scales = const.tile([P, H * E], U8, name="v_scales" + str(b), align_bytes=64)
            nc.vector.quantize_mx(
                out=codes[:].bitcast(FP8X4), scales=scales[:], in_=v_grouped[b][:].rearrange("p n r -> p (n r)")
            )
            v_codes[b] = codes
            v_scales[b] = scales

        turned = {}
        lt = {}
        half = {}
        mixed = {}
        nmax = {}
        expo = {}
        rowsum = {}
        wts = {}
        prod = {}
        upsum = {}
        ub = {}
        uq = {}
        res = {}

        def turn(b, h, name, engine):
            bank = psum.tile([P, SLOTS, P], BF16, name="turn_bank", tag=TURN_TAG, bufs=BUFS[TURN_TAG])
            for r in range(SLOTS):
                nc.tensor.transpose(bank[:, r], raw[name, b, h][:, r], ident_bf[:])
            t = load.tile([P, SLOTS, P], BF16, name="turned_" + name + str(h), tag="turned_" + name + str(h), bufs=2)
            if engine == "v":
                nc.vector.tensor_copy(out=t[:], in_=bank[:])
            else:
                nc.scalar.copy(out=t[:], in_=bank[:])
            turned[name, b, h] = t

        def transpose_qk(s, r):
            n = (s % SLOTS) * 4 + r
            b = s // SLOTS
            if b == 0 or n < 8:
                return
            turn(b, (n - 8) // 2, "k" if n % 2 == 0 else "q", "s")
            if n == 15 and b + 1 < B:
                load_qk(b + 1)

        def logits(s, h, slots):
            b, i = s // SLOTS, s % SLOTS
            if slots[0] == 0:
                lt[s, h] = psum.tile([P, SLOTS, P], F32, name="lt", tag="lt", bufs=BUFS["lt"])
            for x in slots:
                nc.tensor.matmul(
                    out=lt[s, h][:, x],
                    lhsT=turned["k", b, h][:, x],
                    rhs=turned["q", b, h][:, i],
                    start=True,
                    stop=True,
                )

        def logits_a(s, h):
            logits(s, h, (0, 1))

        def logits_b(s, h):
            logits(s, h, (2, 3))

        def scale_first(s, r):
            h = r // 2 * 2
            for j in (r % 2 * 2, r % 2 * 2 + 1):
                t = work.tile([P, SLOTS * P], F32, name="half", tag="half" + str(h) + str(j), bufs=2)
                nc.scalar.activation(
                    out=t[:],
                    in_=lt[s, h][:].rearrange("p r t -> p (r t)"),
                    func=ACT.Copy,
                    scale=wl[:, H * h + j : H * h + j + 1],
                )
                half[s, h, j] = t

        def add_second(s, r):
            h = r // 2 * 2
            for j in (r % 2 * 2, r % 2 * 2 + 1):
                t = half[s, h, j]
                nc.vector.scalar_tensor_tensor(
                    out=t[:],
                    in0=lt[s, h + 1][:].rearrange("p r t -> p (r t)"),
                    scalar=wl[:, H * (h + 1) + j : H * (h + 1) + j + 1],
                    in1=t[:],
                    op0=ALU.mult,
                    op1=ALU.add,
                )

        def mixed_logits(s, j):
            bank = psum.tile([P, SLOTS, P], F32, name="m_bank", tag="m", bufs=BUFS["m"])
            for x in range(SLOTS):
                for h in (0, 2):
                    nc.tensor.matmul(
                        out=bank[:, x],
                        lhsT=half[s, h, j][:, x * P : (x + 1) * P],
                        rhs=ident[:],
                        start=(h == 0),
                        stop=(h == 2),
                        is_transpose=True,
                    )
            mixed[s, j] = bank

        def row_max(s, j):
            if j == 0:
                nmax[s] = work.tile([P, H], F32, name="nmax", tag="nmax", bufs=3)
            nc.vector.tensor_reduce(
                out=nmax[s][:, j : j + 1],
                in_=mixed[s, j][:].rearrange("p r t -> p (r t)"),
                axis=AX.X,
                op=ALU.max,
                negate=True,
            )

        def exponentials(s, j):
            if j == 0:
                rowsum[s] = work.tile([P, H], F32, name="rowsum", tag="rowsum", bufs=3)
            t = work.tile([P, SLOTS * P], F32, name="expo", tag="expo" + str(j), bufs=2)
            nc.scalar.activation(
                out=t[:],
                in_=mixed[s, j][:].rearrange("p r t -> p (r t)"),
                func=ACT.Exp,
                bias=nmax[s][:, j : j + 1],
                accum_out=rowsum[s][:, j : j + 1],
            )
            expo[s, j] = t

        def weights(s, r):
            if r < 3:
                return
            inv = work.tile([P, H], F32, name="inv", tag="inv", bufs=2)
            nc.vector.reciprocal(out=inv[:], in_=rowsum[s][:])
            w = work.tile([P, H, H], F32, name="w", tag="w", bufs=2)
            nc.vector.tensor_tensor(
                out=w[:], in0=wm[:], in1=inv[:].unsqueeze(2).to_broadcast([P, H, H]), op=ALU.mult
            )
            wts[s] = w

        def weighted(s, j):
            for h in range(H):
                t = work.tile([P, SLOTS * P], F32, name="prod", tag="prod" + str(h), bufs=6)
                col = wts[s][:, h, j : j + 1]
                who = who_scales(s, h, j)
                if who == "s":
                    nc.scalar.activation(out=t[:], in_=expo[s, h][:], func=ACT.Copy, scale=col)
                elif who == "v":
                    nc.vector.tensor_scalar(
                        out=t[:], in0=expo[s, h][:], scalar1=col, scalar2=None, op0=ALU.mult
                    )
                else:
                    nc.gpsimd.tensor_scalar(
                        out=t[:], in0=expo[s, h][:], scalar1=col, scalar2=0.0, op0=ALU.mult, op1=ALU.add
                    )
                prod[s, h, j] = t

        def mix_weights(s, j, slots):
            if slots[0] == 0:
                upsum[s, j] = psum.tile([P, SLOTS, P], F32, name="u_bank", tag="u", bufs=BUFS["u"])
            for x in slots:
                for h in range(H):
                    nc.tensor.matmul(
                        out=upsum[s, j][:, x],
                        lhsT=prod[s, h, j][:, x * P : (x + 1) * P],
                        rhs=ident[:],
                        start=(h == 0),
                        stop=(h == H - 1),
                        is_transpose=True,
                    )
                if x == 1:
                    nc.tensor.matmul(
                        out=upsum[s, j][:, 3, :WARM],
                        lhsT=ident[:],
                        rhs=ident[:, :WARM],
                        start=True,
                        stop=True,
                    )

        def mix_weights_a(s, j):
            mix_weights(s, j, (0, 1))

        def mix_weights_b(s, j):
            mix_weights(s, j, (2, 3))

        def gain_stage(s, j):
            if j == 0:
                ub[s] = work.tile([P, H, P, SLOTS], BF16, name="ub", tag="ub", bufs=2, align_bytes=64)
            nc.vector.tensor_tensor(
                out=ub[s][:, j],
                in0=upsum[s, j][:].rearrange("p r t -> p t r"),
                in1=gains[:],
                op=ALU.mult,
            )

        def quantise(s, r):
            if r < 3:
                return
            codes = work.tile([P, H * P], U32, name="u_codes", tag="u_codes", bufs=2, align_bytes=64)
            scales = work.tile([P, H * P], U8, name="u_scales", tag="u_scales", bufs=2, align_bytes=64)
            nc.vector.quantize_mx(
                out=codes[:].bitcast(FP8X4), scales=scales[:], in_=ub[s][:].rearrange("p h t r -> p (h t r)")
            )
            uq[s] = (codes, scales)

        def mx_product(s, r):
            if r < 3:
                return
            b = s // SLOTS
            codes, scales = uq[s]
            bank = psum.tile([P, H, E], F32, name="o_bank", tag=O_TAG, bufs=BUFS[O_TAG])
            for j in range(H):
                nc.tensor.matmul_mx(
                    out=bank[:, j],
                    lhsT=codes[:, j * P : (j + 1) * P].bitcast(FP8X4),
                    lhsT_scale=scales[:, j * P : (j + 1) * P],
                    rhs=v_codes[b][:, j * E : (j + 1) * E].bitcast(FP8X4),
                    rhs_scale=v_scales[b][:, j * E : (j + 1) * E],
                    start=True,
                    stop=True,
                )
            res[s] = bank

        def store(s, r):
            if r < 3:
                return
            b, i = s // SLOTS, s % SLOTS
            t = work.tile([P, H, E], F32, name="o_tile", tag="o_tile", bufs=3)
            nc.scalar.copy(out=t[:], in_=res[s][:])
            nc.sync.dma_start(out=out[b].rearrange("j (p i) e -> p i j e", i=SLOTS)[:, i], in_=t[:])

        for h in range(H):
            turn(0, h, "k", "v")
            turn(0, h, "q", "s")

        stages = {
            "transpose_qk": transpose_qk,
            "logits_a": logits_a,
            "logits_b": logits_b,
            "mx_product": mx_product,
            "mixed_logits": mixed_logits,
            "mix_weights_a": mix_weights_a,
            "mix_weights_b": mix_weights_b,
            "scale_first": scale_first,
            "exponentials": exponentials,
            "weighted": weighted,
            "store": store,
            "gain": gain_stage,
            "row_max": row_max,
            "add_second": add_second,
            "weights": weights,
            "quantise": quantise,
        }
        first = min(offset for name, offset in ORDER)
        last = max(offset for name, offset in ORDER)
        for g in range(first, 4 * STEPS + last):
            for stage, offset in ((widen_v, V_AT), (group_v, V_AT + 1), (quantise_v, V_AT + 3)):
                if (g - offset) % V_EVERY == 0 and 0 <= (g - offset) // V_EVERY < B:
                    stage((g - offset) // V_EVERY)
            for name, offset in ORDER:
                n = g - offset
                if 0 <= n < 4 * STEPS:
                    stages[name](n // 4, n % 4)
